import numpy as np
import ml_dtypes


def mxq(x, axis, fmt="e4m3"):
    dtype, down = {"e4m3": (ml_dtypes.float8_e4m3fn, 7), "e5m2": (ml_dtypes.float8_e5m2, 14)}[fmt]
    v = np.moveaxis(np.asarray(x, np.float32).astype(ml_dtypes.bfloat16).astype(np.float64), axis, -1)
    blocks = v.reshape(v.shape[:-1] + (-1, 32))
    amax = np.abs(blocks).max(-1, keepdims=True)
    byte = np.maximum(np.where(amax > 0, np.frexp(amax)[1] - 1 + 127, 0) - down, 1)
    scale = np.exp2(byte - 127.0)
    codes = (blocks / scale).astype(np.float32).astype(dtype).astype(np.float64)
    return np.moveaxis((codes * scale).reshape(v.shape), -1, axis)


WIDE = False


def mx_kscale(k):
    if not WIDE:
        return np.ones(k)
    levels = np.array([10, -10, 5, -5, 0])
    if k % 512:
        return np.exp2(np.random.permutation(np.resize(levels, k // 32))).repeat(32)
    a = np.empty((k // 512, 16))
    for p in range(k // 512):
        a[p, :8] = np.random.permutation(np.resize(levels, 8))
        for g in range(8):
            far = levels[np.abs(levels - a[p, g]) >= 10]
            a[p, g + 8] = far[np.random.randint(len(far))]
    return np.exp2(a.ravel()).repeat(32)


def f64(x):
    return np.asarray(x).astype(np.float64)


def striped(idx):
    return np.tile(idx.reshape(-1, 16).T, (8, 1)).astype(np.uint16)


def unstriped(offs):
    return offs[:16].T.reshape(-1).astype(np.int64)


def pack_weight(w):
    k, n = w.shape
    w = f64(np.asarray(w, np.float32).astype(ml_dtypes.bfloat16)).reshape(k // 32, 32, n)
    amax = np.abs(w).max(1)
    byte = np.clip(np.where(amax > 0, np.frexp(amax)[1] - 1 + 127 - 7, 1), 1, 254)
    scaled = (w * np.exp2(127.0 - byte)[:, None, :]).reshape(k, n).astype(np.float32)
    words = np.ascontiguousarray(scaled.reshape(k // 512, 128, 4, n).transpose(0, 1, 3, 2)).astype(ml_dtypes.float8_e4m3fn).view(np.uint8)
    return words, np.ascontiguousarray(byte.astype(np.uint8).reshape(k // 512, 16, n))


def unpack_weight(words, scales):
    g, p, n, _ = words.shape
    vals = np.ascontiguousarray(words).view(ml_dtypes.float8_e4m3fn).astype(np.float64) * np.repeat(np.exp2(scales.astype(np.float64) - 127.0), 8, axis=1)[..., None]
    return vals.transpose(0, 1, 3, 2).reshape(g * 512, n)


def relu(v):
    return np.maximum(v, 0.0)


K, T, S, N, H, W = 512, 1024, 512, 128, 512, 2048


def setup_inputs():
    n = np.random.standard_normal
    s = mx_kscale(K)[:, None]
    u = mx_kscale(H)
    packed_xT = pack_weight(n((K, T)) * s)
    packed_eT = pack_weight(n((K, W)) * s)
    return {
        "x_words": packed_xT[0],
        "x_scales": packed_xT[1],
        "w1": (n((K, H)) / np.sqrt(K) / s).astype(np.float32),
        "e_words": packed_eT[0],
        "e_scales": packed_eT[1],
        "w2": (n((K, H)) / np.sqrt(K) / s).astype(np.float32),
        "thr": (-np.random.uniform(0.2, 0.8, (H, 1))).astype(np.float32),
        "unit": (np.random.uniform(0.6, 1.4, (H, 1)) * u[:, None]).astype(np.float32),
        "w3": (n((H, N)) / np.sqrt(H) / u[:, None]).astype(np.float32),
        "tgt": (n((N, S))).astype(np.float32),
        "offs": striped(np.random.permutation(T)[:S]),
        "mate": striped(np.random.permutation(W)[:S]),
        "fold": striped(np.random.permutation(S)),
    }


def reference(x_words, x_scales, w1, e_words, e_scales, w2, thr, unit, w3, tgt, offs, mate, fold):
    xq = unpack_weight(x_words, x_scales)[:, unstriped(offs)]
    y = mxq(f64(w1), 0, "e4m3").T @ xq
    e_mate = unpack_weight(e_words, e_scales)[:, unstriped(mate)]
    ye = mxq(f64(w2), 0, "e4m3").T @ e_mate
    lat = relu(y + ye + f64(thr))
    ff = lat[:, unstriped(fold)]
    mx = np.maximum(lat, 0.8 * ff)
    hid = f64(unit) * mx
    rr = mxq(f64(w3), 0, "e4m3").T @ mxq(hid, 0, "e4m3")
    er = f64(tgt) - rr
    return np.abs(er) - (0.3 * rr)

@@ -1,0 +1,190 @@
+from contextlib import ExitStack
+
+import concourse.mybir as mybir
+
+F32 = mybir.dt.float32
+BF16 = mybir.dt.bfloat16
+I32 = mybir.dt.int32
+U32 = mybir.dt.uint32
+U16 = mybir.dt.uint16
+U8 = mybir.dt.uint8
+FP8X4 = mybir.dt.float8_e4m3fn_x4
+ALU = mybir.AluOpType
+ACT = mybir.ActivationFunctionType
+
+K, T, S, N, H, W = 512, 1024, 512, 128, 512, 2048
+FLOPS = 2 * K * H * S * 2 + 2 * H * N * S
+
+P = 128
+PACK = 4
+HALF = S // 2
+CHUNKS = ((0, 256), (256, 512))
+
+
+def tile_picked_ysaecr_rec_p_kernel(
+    tc, x_words, x_scales, w1, e_words, e_scales, w2, thr, unit, w3, tgt, offs, mate, fold, out
+):
+    nc = tc.nc
+    with ExitStack() as ctx:
+        keep = ctx.enter_context(tc.tile_pool(name="keep", bufs=1))
+        psum = ctx.enter_context(tc.psum_pool(name="psum", bufs=1))
+
+        def sb(name, shape, dtype, tag=None):
+            return keep.tile(shape, dtype, name=name, tag=tag or name, align_bytes=64)
+
+        def entries(list_tile, lo, hi):
+            return list_tile[:, lo // 16 : hi // 16]
+
+        x_plane = sb("x_plane", [P, T], U8)
+        e_plane = sb("e_plane", [P, W], U8)
+        nc.vector.memset(x_plane[:].bitcast(I32), 0)
+        nc.vector.memset(e_plane[:].bitcast(I32), 0)
+
+        offs_sb = keep.tile([P, S // 16], U16, name="offs_sb")
+        mate_sb = keep.tile([P, S // 16], U16, name="mate_sb")
+        fold_sb = keep.tile([P, S // 16], U16, name="fold_sb")
+        nc.sync.dma_start(offs_sb[:], offs)
+        nc.sync.dma_start(mate_sb[:], mate)
+        nc.sync.dma_start(fold_sb[:], fold)
+
+        w1_raw = sb("w1_raw", [P, PACK, H], F32, tag="staging")
+        w2_raw = sb("w2_raw", [P, PACK, H], F32)
+        x_table = sb("x_table", [P, T], U32)
+        e_table = sb("e_table", [P, W], U32)
+        nc.sync.dma_start(w1_raw[:], w1.rearrange("(p j) c -> p j c", j=PACK))
+        nc.sync.dma_start(x_table[:].bitcast(I32), x_words[0].rearrange("p n r -> p (n r)").bitcast(I32))
+        for q in range(4):
+            nc.scalar.dma_start(x_plane[32 * q : 32 * q + 4, :].bitcast(I32), x_scales[0, 4 * q : 4 * q + 4, :].bitcast(I32))
+        nc.sync.dma_start(w2_raw[:], w2.rearrange("(p j) c -> p j c", j=PACK))
+        nc.sync.dma_start(e_table[:].bitcast(I32), e_words[0].rearrange("p n r -> p (n r)").bitcast(I32))
+
+        unit_sb = sb("unit_sb", [P, PACK], F32)
+        thr_sb = sb("thr_sb", [P, PACK], F32)
+        nc.gpsimd.dma_start(unit_sb[:], unit.rearrange("(p t) o -> p (t o)", t=PACK))
+        nc.gpsimd.dma_start(thr_sb[:], thr.rearrange("(p t) o -> p (t o)", t=PACK))
+        for q in range(4):
+            nc.gpsimd.dma_start(e_plane[32 * q : 32 * q + 4, :].bitcast(I32), e_scales[0, 4 * q : 4 * q + 4, :].bitcast(I32))
+
+        own_scale = sb("own_scale", [P, PACK], F32)
+        mate_scale = sb("mate_scale", [P, PACK], F32)
+        unit_sign = sb("unit_sign", [P, PACK], F32)
+        own_bias = sb("own_bias", [P, PACK], F32)
+        mate_bias = sb("mate_bias", [P, PACK], F32)
+        nc.scalar.activation(own_scale[:], unit_sb[:], ACT.Abs)
+        nc.scalar.activation(mate_scale[:], unit_sb[:], ACT.Abs, scale=0.8)
+        nc.scalar.activation(unit_sign[:], unit_sb[:], ACT.Sign)
+        nc.gpsimd.tensor_tensor(own_bias[:], own_scale[:], thr_sb[:], ALU.mult)
+        nc.gpsimd.tensor_tensor(mate_bias[:], mate_scale[:], thr_sb[:], ALU.mult)
+
+        x_codes = sb("x_codes", [P, S], U32)
+        x_bytes = sb("x_bytes", [P, S], U8)
+        e_codes = sb("e_codes", [P, S], U32)
+        e_bytes = sb("e_bytes", [P, S], U8)
+        nc.vector.tensor_copy(x_bytes[:], x_plane[:].indirect(offs_sb[:]))
+        nc.vector.tensor_copy(x_codes[:], x_table[:].indirect(offs_sb[:]))
+        nc.vector.tensor_copy(e_bytes[:], e_plane[:].indirect(mate_sb[:]))
+
+        w1_bf = sb("w1_bf", [P, PACK * H], BF16)
+        nc.scalar.copy(
+            w1_bf[:].rearrange("p (t m j) -> p m j t", t=PACK, j=PACK),
+            w1_raw[:].rearrange("p j (m t) -> p m j t", t=PACK),
+        )
+        w1_codes = sb("w1_codes", [P, H], U32)
+        w1_bytes = sb("w1_bytes", [P, H], U8)
+        nc.vector.quantize_mx(out=w1_codes[:].bitcast(FP8X4), scales=w1_bytes[:], in_=w1_bf[:])
+
+        late = sb("late", [P, 2, S], F32, tag="staging")
+        w3_raw = late[:, 0, :].rearrange("p (j n) -> p j n", j=PACK)
+        tgt_sb = late[:, 1, :]
+        nc.sync.dma_start(w3_raw, w3.rearrange("(p j) n -> p j n", j=PACK))
+        nc.sync.dma_start(tgt_sb, tgt)
+
+        w2_codes = sb("w2_codes", [P, H], U32)
+        w2_bytes = sb("w2_bytes", [P, H], U8)
+        w2_dealt = w2_raw[:].rearrange("p j (m t) -> p m j t", t=PACK)
+        for u, cast in enumerate((nc.vector.tensor_copy, nc.scalar.copy)):
+            w2_bf = sb("w2_bf%d" % u, [P, 2 * H], BF16)
+            cast(w2_bf[:].rearrange("p (t m j) -> p m j t", t=2, j=PACK), w2_dealt[:, :, :, 2 * u : 2 * u + 2])
+            cols = slice(u * H // 2, (u + 1) * H // 2)
+            nc.vector.quantize_mx(out=w2_codes[:, cols].bitcast(FP8X4), scales=w2_bytes[:, cols], in_=w2_bf[:])
+
+        pieces = [(0, 0, HALF), (0, HALF, S)] + [(t, 0, S) for t in range(1, PACK)]
+        banks = [psum.tile([P, hi - lo], F32, name="z%d" % i) for i, (t, lo, hi) in enumerate(pieces)]
+
+        def encode(bank, t, lo, hi, w_codes, w_bytes, codes, scale_bytes, first):
+            rows = slice(t * P, (t + 1) * P)
+            nc.tensor.matmul_mx(
+                out=bank[:],
+                lhsT=w_codes[:, rows].bitcast(FP8X4),
+                lhsT_scale=w_bytes[:, rows],
+                rhs=codes[:, lo:hi].bitcast(FP8X4),
+                rhs_scale=scale_bytes[:, lo:hi],
+                start=first,
+                stop=not first,
+            )
+
+        for bank, (t, lo, hi) in zip(banks, pieces):
+            encode(bank, t, lo, hi, w1_codes, w1_bytes, x_codes, x_bytes, True)
+        for lo, hi in ((0, HALF), (HALF, S)):
+            nc.vector.tensor_copy(e_codes[:, lo:hi], e_table[:].indirect(entries(mate_sb, lo, hi)))
+        for bank, (t, lo, hi) in zip(banks, pieces):
+            encode(bank, t, lo, hi, w2_codes, w2_bytes, e_codes, e_bytes, False)
+
+        windows = [sb("window%d" % t, [P, S], F32) for t in range(PACK)]
+        own = sb("own", [P, PACK, S], F32)
+        fetched = sb("fetched", [P, PACK, S], F32)
+        for bank, (t, lo, hi) in zip(banks, pieces):
+            nc.scalar.activation(windows[t][:, lo:hi], bank[:], ACT.Relu, bias=mate_bias[:, t : t + 1], scale=mate_scale[:, t : t + 1])
+        for bank, (t, lo, hi) in zip(banks, pieces):
+            nc.scalar.activation(own[:, t, lo:hi], bank[:], ACT.Relu, bias=own_bias[:, t : t + 1], scale=own_scale[:, t : t + 1])
+        for t in range(PACK):
+            for lo, hi in ((0, HALF), (HALF, S)):
+                nc.vector.tensor_copy(fetched[:, t, lo:hi], windows[t][:].indirect(entries(fold_sb, lo, hi)))
+
+        w3_signed = sb("w3_signed", [P, PACK, N], F32)
+        for j in range(PACK):
+            nc.scalar.activation(w3_signed[:, j, :], w3_raw[:, j, :], ACT.Copy, scale=unit_sign[:, j : j + 1])
+        w3_bf = sb("w3_bf", [P, N * PACK], BF16)
+        nc.scalar.copy(
+            w3_bf[:].rearrange("p (c i j) -> p c j i", i=4, j=PACK),
+            w3_signed[:].rearrange("p j (c i) -> p c j i", i=4),
+        )
+        w3_codes = sb("w3_codes", [P, N], U32)
+        w3_bytes = sb("w3_bytes", [P, N], U8)
+        nc.vector.quantize_mx(out=w3_codes[:].bitcast(FP8X4), scales=w3_bytes[:], in_=w3_bf[:])
+
+        rebuilt = []
+        for c, (lo, hi) in enumerate(CHUNKS):
+            n = hi - lo
+            hid_bf = sb("hid_bf%d" % c, [P, n * PACK], BF16)
+            nc.vector.tensor_tensor(
+                hid_bf[:].rearrange("p (c i t) -> p c t i", i=4, t=PACK),
+                fetched[:, :, lo:hi].rearrange("p t (c i) -> p c t i", i=4),
+                own[:, :, lo:hi].rearrange("p t (c i) -> p c t i", i=4),
+                ALU.max,
+            )
+            hid_codes = sb("hid_codes%d" % c, [P, n], U32)
+            hid_bytes = sb("hid_bytes%d" % c, [P, n], U8)
+            nc.vector.quantize_mx(out=hid_codes[:].bitcast(FP8X4), scales=hid_bytes[:], in_=hid_bf[:])
+            rr = psum.tile([P, n], F32, name="rr%d" % c)
+            nc.tensor.matmul_mx(
+                out=rr[:],
+                lhsT=w3_codes[:].bitcast(FP8X4),
+                lhsT_scale=w3_bytes[:],
+                rhs=hid_codes[:].bitcast(FP8X4),
+                rhs_scale=hid_bytes[:],
+                start=True,
+                stop=True,
+            )
+            rebuilt.append(rr)
+
+        for c, (lo, hi) in enumerate(CHUNKS):
+            n = hi - lo
+            rr = rebuilt[c]
+            err = sb("err%d" % c, [P, n], F32)
+            size = sb("size%d" % c, [P, n], F32)
+            result = sb("result%d" % c, [P, n], F32)
+            nc.vector.scalar_tensor_tensor(err[:], rr[:], -1.0, tgt_sb[:, lo:hi], ALU.mult, ALU.add)
+            nc.scalar.activation(size[:], err[:], ACT.Abs)
+            nc.vector.scalar_tensor_tensor(result[:], rr[:], -0.3, size[:], ALU.mult, ALU.add)
+            nc.sync.dma_start(out[:, lo:hi], result[:])

@@ -37,33 +37,37 @@ def tile_picked_ysaecr_rec_p_kernel(
 
         x_plane = sb("x_plane", [P, T], U8)
         e_plane = sb("e_plane", [P, W], U8)
-        nc.vector.memset(x_plane[:].bitcast(I32), 0)
-        nc.vector.memset(e_plane[:].bitcast(I32), 0)
+        nc.gpsimd.memset(x_plane[:].bitcast(I32), 0)
+        nc.gpsimd.memset(e_plane[:].bitcast(I32), 0)
+
+        def load_scale_rows(plane, rows):
+            for q in range(4):
+                nc.sync.dma_start(plane[32 * q : 32 * q + 4, :].bitcast(I32), rows[0, 4 * q : 4 * q + 4, :].bitcast(I32))
 
         offs_sb = keep.tile([P, S // 16], U16, name="offs_sb")
         mate_sb = keep.tile([P, S // 16], U16, name="mate_sb")
         fold_sb = keep.tile([P, S // 16], U16, name="fold_sb")
-        nc.sync.dma_start(offs_sb[:], offs)
-        nc.sync.dma_start(mate_sb[:], mate)
-        nc.sync.dma_start(fold_sb[:], fold)
-
-        w1_raw = sb("w1_raw", [P, PACK, H], F32, tag="staging")
+        unit_sb = sb("unit_sb", [P, PACK], F32)
+        thr_sb = sb("thr_sb", [P, PACK], F32)
+        w1_raw = sb("w1_raw", [P, PACK, H], F32)
         w2_raw = sb("w2_raw", [P, PACK, H], F32)
         x_table = sb("x_table", [P, T], U32)
         e_table = sb("e_table", [P, W], U32)
-        nc.sync.dma_start(w1_raw[:], w1.rearrange("(p j) c -> p j c", j=PACK))
+        nc.sync.dma_start(offs_sb[:], offs)
+        nc.sync.dma_start(mate_sb[:], mate)
         nc.sync.dma_start(x_table[:].bitcast(I32), x_words[0].rearrange("p n r -> p (n r)").bitcast(I32))
-        for q in range(4):
-            nc.scalar.dma_start(x_plane[32 * q : 32 * q + 4, :].bitcast(I32), x_scales[0, 4 * q : 4 * q + 4, :].bitcast(I32))
+        load_scale_rows(x_plane, x_scales)
+        nc.sync.dma_start(w1_raw[:], w1.rearrange("(p j) c -> p j c", j=PACK))
+        load_scale_rows(e_plane, e_scales)
         nc.sync.dma_start(w2_raw[:], w2.rearrange("(p j) c -> p j c", j=PACK))
         nc.sync.dma_start(e_table[:].bitcast(I32), e_words[0].rearrange("p n r -> p (n r)").bitcast(I32))
-
-        unit_sb = sb("unit_sb", [P, PACK], F32)
-        thr_sb = sb("thr_sb", [P, PACK], F32)
         nc.gpsimd.dma_start(unit_sb[:], unit.rearrange("(p t) o -> p (t o)", t=PACK))
         nc.gpsimd.dma_start(thr_sb[:], thr.rearrange("(p t) o -> p (t o)", t=PACK))
-        for q in range(4):
-            nc.gpsimd.dma_start(e_plane[32 * q : 32 * q + 4, :].bitcast(I32), e_scales[0, 4 * q : 4 * q + 4, :].bitcast(I32))
+        w3_raw = sb("w3_raw", [P, PACK, N], F32, tag="w3_then_fetched")
+        tgt_sb = sb("tgt_sb", [P, S], F32)
+        nc.sync.dma_start(w3_raw[:], w3.rearrange("(p j) n -> p j n", j=PACK))
+        nc.sync.dma_start(fold_sb[:], fold)
+        nc.sync.dma_start(tgt_sb[:], tgt)
 
         own_scale = sb("own_scale", [P, PACK], F32)
         mate_scale = sb("mate_scale", [P, PACK], F32)
@@ -80,8 +84,8 @@ def tile_picked_ysaecr_rec_p_kernel(
         x_bytes = sb("x_bytes", [P, S], U8)
         e_codes = sb("e_codes", [P, S], U32)
         e_bytes = sb("e_bytes", [P, S], U8)
-        nc.vector.tensor_copy(x_bytes[:], x_plane[:].indirect(offs_sb[:]))
         nc.vector.tensor_copy(x_codes[:], x_table[:].indirect(offs_sb[:]))
+        nc.vector.tensor_copy(x_bytes[:], x_plane[:].indirect(offs_sb[:]))
         nc.vector.tensor_copy(e_bytes[:], e_plane[:].indirect(mate_sb[:]))
 
         w1_bf = sb("w1_bf", [P, PACK * H], BF16)
@@ -93,11 +97,6 @@ def tile_picked_ysaecr_rec_p_kernel(
         w1_bytes = sb("w1_bytes", [P, H], U8)
         nc.vector.quantize_mx(out=w1_codes[:].bitcast(FP8X4), scales=w1_bytes[:], in_=w1_bf[:])
 
-        late = sb("late", [P, 2, S], F32, tag="staging")
-        w3_raw = late[:, 0, :].rearrange("p (j n) -> p j n", j=PACK)
-        tgt_sb = late[:, 1, :]
-        nc.sync.dma_start(w3_raw, w3.rearrange("(p j) n -> p j n", j=PACK))
-        nc.sync.dma_start(tgt_sb, tgt)
 
         w2_codes = sb("w2_codes", [P, H], U32)
         w2_bytes = sb("w2_bytes", [P, H], U8)
@@ -130,28 +129,31 @@ def tile_picked_ysaecr_rec_p_kernel(
         for bank, (t, lo, hi) in zip(banks, pieces):
             encode(bank, t, lo, hi, w2_codes, w2_bytes, e_codes, e_bytes, False)
 
-        windows = [sb("window%d" % t, [P, S], F32) for t in range(PACK)]
-        own = sb("own", [P, PACK, S], F32)
-        fetched = sb("fetched", [P, PACK, S], F32)
-        for bank, (t, lo, hi) in zip(banks, pieces):
-            nc.scalar.activation(windows[t][:, lo:hi], bank[:], ACT.Relu, bias=mate_bias[:, t : t + 1], scale=mate_scale[:, t : t + 1])
-        for bank, (t, lo, hi) in zip(banks, pieces):
-            nc.scalar.activation(own[:, t, lo:hi], bank[:], ACT.Relu, bias=own_bias[:, t : t + 1], scale=own_scale[:, t : t + 1])
-        for t in range(PACK):
-            for lo, hi in ((0, HALF), (HALF, S)):
-                nc.vector.tensor_copy(fetched[:, t, lo:hi], windows[t][:].indirect(entries(fold_sb, lo, hi)))
-
-        w3_signed = sb("w3_signed", [P, PACK, N], F32)
-        for j in range(PACK):
-            nc.scalar.activation(w3_signed[:, j, :], w3_raw[:, j, :], ACT.Copy, scale=unit_sign[:, j : j + 1])
         w3_bf = sb("w3_bf", [P, N * PACK], BF16)
-        nc.scalar.copy(
+        nc.vector.tensor_tensor(
             w3_bf[:].rearrange("p (c i j) -> p c j i", i=4, j=PACK),
-            w3_signed[:].rearrange("p j (c i) -> p c j i", i=4),
+            w3_raw[:].rearrange("p j (c i) -> p c j i", i=4),
+            unit_sign[:].unsqueeze(1).unsqueeze(3).broadcast_to([P, N // 4, PACK, 4]),
+            ALU.mult,
         )
         w3_codes = sb("w3_codes", [P, N], U32)
         w3_bytes = sb("w3_bytes", [P, N], U8)
         nc.vector.quantize_mx(out=w3_codes[:].bitcast(FP8X4), scales=w3_bytes[:], in_=w3_bf[:])
+
+        rival = sb("rival", [P, PACK * S], F32)
+
+        def rival_at(t):
+            return (PACK - 1 - t) * S
+
+        own = sb("own", [P, PACK, S], F32)
+        fetched = sb("fetched", [P, PACK, S], F32, tag="w3_then_fetched")
+        for bank, (t, lo, hi) in zip(banks, pieces):
+            nc.scalar.activation(rival[:, rival_at(t) + lo : rival_at(t) + hi], bank[:], ACT.Relu, bias=mate_bias[:, t : t + 1], scale=mate_scale[:, t : t + 1])
+        for bank, (t, lo, hi) in zip(banks, pieces):
+            nc.scalar.activation(own[:, t, lo:hi], bank[:], ACT.Relu, bias=own_bias[:, t : t + 1], scale=own_scale[:, t : t + 1])
+        for t, lo, hi in pieces:
+            window = rival[:, rival_at(t) : rival_at(t) + 2 * (hi - lo)]
+            nc.vector.tensor_copy(fetched[:, t, lo:hi], window.indirect(entries(fold_sb, lo, hi)))
 
         rebuilt = []
         for c, (lo, hi) in enumerate(CHUNKS):

@@ -17,8 +17,13 @@ FLOPS = 2 * K * H * S * 2 + 2 * H * N * S
 
 P = 128
 PACK = 4
+QUADRANTS = 4
+LIST_ROWS = 16
 HALF = S // 2
-CHUNKS = ((0, 256), (256, 512))
+LOWER, UPPER, WHOLE = (0, HALF), (HALF, S), (0, S)
+PARTNER = 0.8
+UNDO_PARTNER = 1.25
+REBUILT = 0.3
 
 
 def tile_picked_ysaecr_rec_p_kernel(
@@ -33,107 +38,106 @@ def tile_picked_ysaecr_rec_p_kernel(
             return keep.tile(shape, dtype, name=name, tag=tag or name, align_bytes=64)
 
         def entries(list_tile, lo, hi):
-            return list_tile[:, lo // 16 : hi // 16]
+            return list_tile[:, lo // LIST_ROWS : hi // LIST_ROWS]
+
+        def load_words(table, words):
+            nc.sync.dma_start(table[:].bitcast(I32), words[0].rearrange("p n j -> p (n j)").bitcast(I32))
+
+        def load_scale_rows(plane, rows):
+            for q in range(QUADRANTS):
+                nc.sync.dma_start(plane[32 * q : 32 * q + 4, :].bitcast(I32), rows[0, 4 * q : 4 * q + 4, :].bitcast(I32))
+
+        def by_pairs(planes):
+            return planes.rearrange("p t (c i) -> p c t i", i=2)
+
+        def woven(tile):
+            return tile[:].rearrange("p (c i t) -> p c t i", i=2, t=PACK)
 
         x_plane = sb("x_plane", [P, T], U8)
         e_plane = sb("e_plane", [P, W], U8)
         nc.gpsimd.memset(x_plane[:].bitcast(I32), 0)
-        nc.gpsimd.memset(e_plane[:].bitcast(I32), 0)
+        nc.vector.memset(e_plane[:].bitcast(I32), 0)
 
-        def load_scale_rows(plane, rows):
-            for q in range(4):
-                nc.sync.dma_start(plane[32 * q : 32 * q + 4, :].bitcast(I32), rows[0, 4 * q : 4 * q + 4, :].bitcast(I32))
-
-        offs_sb = keep.tile([P, S // 16], U16, name="offs_sb")
-        mate_sb = keep.tile([P, S // 16], U16, name="mate_sb")
-        fold_sb = keep.tile([P, S // 16], U16, name="fold_sb")
+        offs_sb = keep.tile([P, S // LIST_ROWS], U16, name="offs_sb")
+        mate_sb = keep.tile([P, S // LIST_ROWS], U16, name="mate_sb")
+        fold_sb = keep.tile([P, S // LIST_ROWS], U16, name="fold_sb")
         unit_sb = sb("unit_sb", [P, PACK], F32)
         thr_sb = sb("thr_sb", [P, PACK], F32)
-        w1_raw = sb("w1_raw", [P, PACK, H], F32)
-        w2_raw = sb("w2_raw", [P, PACK, H], F32)
-        x_table = sb("x_table", [P, T], U32)
-        e_table = sb("e_table", [P, W], U32)
+        w1_raw = sb("w1_raw", [P, PACK, H], F32, tag="w1_then_w3")
+        w2_raw = sb("w2_raw", [P, PACK, H], F32, tag="w2_then_tgt")
+        x_table = sb("x_table", [P, T], U32, tag="x_then_e")
+        load_words(x_table, x_words)
         nc.sync.dma_start(offs_sb[:], offs)
         nc.sync.dma_start(mate_sb[:], mate)
-        nc.sync.dma_start(x_table[:].bitcast(I32), x_words[0].rearrange("p n r -> p (n r)").bitcast(I32))
         load_scale_rows(x_plane, x_scales)
         nc.sync.dma_start(w1_raw[:], w1.rearrange("(p j) c -> p j c", j=PACK))
+        nc.sync.dma_start(fold_sb[:], fold)
         load_scale_rows(e_plane, e_scales)
         nc.sync.dma_start(w2_raw[:], w2.rearrange("(p j) c -> p j c", j=PACK))
-        nc.sync.dma_start(e_table[:].bitcast(I32), e_words[0].rearrange("p n r -> p (n r)").bitcast(I32))
         nc.gpsimd.dma_start(unit_sb[:], unit.rearrange("(p t) o -> p (t o)", t=PACK))
         nc.gpsimd.dma_start(thr_sb[:], thr.rearrange("(p t) o -> p (t o)", t=PACK))
-        w3_raw = sb("w3_raw", [P, PACK, N], F32, tag="w3_then_fetched")
-        tgt_sb = sb("tgt_sb", [P, S], F32)
-        nc.sync.dma_start(w3_raw[:], w3.rearrange("(p j) n -> p j n", j=PACK))
-        nc.sync.dma_start(fold_sb[:], fold)
-        nc.sync.dma_start(tgt_sb[:], tgt)
 
-        own_scale = sb("own_scale", [P, PACK], F32)
-        mate_scale = sb("mate_scale", [P, PACK], F32)
+        rival_scale = sb("rival_scale", [P, PACK], F32)
         unit_sign = sb("unit_sign", [P, PACK], F32)
-        own_bias = sb("own_bias", [P, PACK], F32)
-        mate_bias = sb("mate_bias", [P, PACK], F32)
-        nc.scalar.activation(own_scale[:], unit_sb[:], ACT.Abs)
-        nc.scalar.activation(mate_scale[:], unit_sb[:], ACT.Abs, scale=0.8)
+        rival_bias = sb("rival_bias", [P, PACK], F32)
+        nc.scalar.activation(rival_scale[:], unit_sb[:], ACT.Abs, scale=PARTNER)
         nc.scalar.activation(unit_sign[:], unit_sb[:], ACT.Sign)
-        nc.gpsimd.tensor_tensor(own_bias[:], own_scale[:], thr_sb[:], ALU.mult)
-        nc.gpsimd.tensor_tensor(mate_bias[:], mate_scale[:], thr_sb[:], ALU.mult)
+        nc.gpsimd.tensor_tensor(rival_bias[:], rival_scale[:], thr_sb[:], ALU.mult)
 
         x_codes = sb("x_codes", [P, S], U32)
         x_bytes = sb("x_bytes", [P, S], U8)
         e_codes = sb("e_codes", [P, S], U32)
         e_bytes = sb("e_bytes", [P, S], U8)
         nc.vector.tensor_copy(x_codes[:], x_table[:].indirect(offs_sb[:]))
+        e_table = sb("e_table", [P, W], U32, tag="x_then_e")
+        load_words(e_table, e_words)
         nc.vector.tensor_copy(x_bytes[:], x_plane[:].indirect(offs_sb[:]))
+
+        def quantize_encoder(name, raw):
+            codes = sb(name + "_codes", [P, H], U32)
+            scale_bytes = sb(name + "_bytes", [P, H], U8)
+            dealt = raw[:].rearrange("p j (m t) -> p m j t", t=PACK)
+            for pair, cast in ((1, nc.vector.tensor_copy), (0, nc.scalar.copy)):
+                rounded = sb("%s_bf%d" % (name, pair), [P, 2 * H], BF16)
+                cast(rounded[:].rearrange("p (t m j) -> p m j t", t=2, j=PACK), dealt[:, :, :, 2 * pair : 2 * pair + 2])
+                cols = slice(pair * H // 2, (pair + 1) * H // 2)
+                nc.vector.quantize_mx(out=codes[:, cols].bitcast(FP8X4), scales=scale_bytes[:, cols], in_=rounded[:])
+            return codes, scale_bytes
+
+        w1_codes, w1_bytes = quantize_encoder("w1", w1_raw)
+        w3_raw = sb("w3_raw", [P, PACK, N], F32, tag="w1_then_w3")
+        nc.sync.dma_start(w3_raw[:], w3.rearrange("(p j) n -> p j n", j=PACK))
+        w2_codes, w2_bytes = quantize_encoder("w2", w2_raw)
+        tgt_sb = sb("tgt_sb", [P, S], F32, tag="w2_then_tgt")
+        nc.sync.dma_start(tgt_sb[:], tgt)
         nc.vector.tensor_copy(e_bytes[:], e_plane[:].indirect(mate_sb[:]))
 
-        w1_bf = sb("w1_bf", [P, PACK * H], BF16)
-        nc.scalar.copy(
-            w1_bf[:].rearrange("p (t m j) -> p m j t", t=PACK, j=PACK),
-            w1_raw[:].rearrange("p j (m t) -> p m j t", t=PACK),
-        )
-        w1_codes = sb("w1_codes", [P, H], U32)
-        w1_bytes = sb("w1_bytes", [P, H], U8)
-        nc.vector.quantize_mx(out=w1_codes[:].bitcast(FP8X4), scales=w1_bytes[:], in_=w1_bf[:])
-
-
-        w2_codes = sb("w2_codes", [P, H], U32)
-        w2_bytes = sb("w2_bytes", [P, H], U8)
-        w2_dealt = w2_raw[:].rearrange("p j (m t) -> p m j t", t=PACK)
-        for u, cast in enumerate((nc.vector.tensor_copy, nc.scalar.copy)):
-            w2_bf = sb("w2_bf%d" % u, [P, 2 * H], BF16)
-            cast(w2_bf[:].rearrange("p (t m j) -> p m j t", t=2, j=PACK), w2_dealt[:, :, :, 2 * u : 2 * u + 2])
-            cols = slice(u * H // 2, (u + 1) * H // 2)
-            nc.vector.quantize_mx(out=w2_codes[:, cols].bitcast(FP8X4), scales=w2_bytes[:, cols], in_=w2_bf[:])
-
-        pieces = [(0, 0, HALF), (0, HALF, S)] + [(t, 0, S) for t in range(1, PACK)]
+        pieces = [(PACK - 1, *LOWER), (PACK - 1, *UPPER)] + [(t, *WHOLE) for t in reversed(range(PACK - 1))]
         banks = [psum.tile([P, hi - lo], F32, name="z%d" % i) for i, (t, lo, hi) in enumerate(pieces)]
 
-        def encode(bank, t, lo, hi, w_codes, w_bytes, codes, scale_bytes, first):
-            rows = slice(t * P, (t + 1) * P)
-            nc.tensor.matmul_mx(
-                out=bank[:],
-                lhsT=w_codes[:, rows].bitcast(FP8X4),
-                lhsT_scale=w_bytes[:, rows],
-                rhs=codes[:, lo:hi].bitcast(FP8X4),
-                rhs_scale=scale_bytes[:, lo:hi],
-                start=first,
-                stop=not first,
-            )
+        def encode(w_codes, w_bytes, codes, scale_bytes, first):
+            for bank, (t, lo, hi) in zip(banks, pieces):
+                latents = slice(t * P, (t + 1) * P)
+                nc.tensor.matmul_mx(
+                    out=bank[:],
+                    lhsT=w_codes[:, latents].bitcast(FP8X4),
+                    lhsT_scale=w_bytes[:, latents],
+                    rhs=codes[:, lo:hi].bitcast(FP8X4),
+                    rhs_scale=scale_bytes[:, lo:hi],
+                    start=first,
+                    stop=not first,
+                )
 
-        for bank, (t, lo, hi) in zip(banks, pieces):
-            encode(bank, t, lo, hi, w1_codes, w1_bytes, x_codes, x_bytes, True)
-        for lo, hi in ((0, HALF), (HALF, S)):
+        encode(w1_codes, w1_bytes, x_codes, x_bytes, first=True)
+        for lo, hi in (LOWER, UPPER):
             nc.vector.tensor_copy(e_codes[:, lo:hi], e_table[:].indirect(entries(mate_sb, lo, hi)))
-        for bank, (t, lo, hi) in zip(banks, pieces):
-            encode(bank, t, lo, hi, w2_codes, w2_bytes, e_codes, e_bytes, False)
+        encode(w2_codes, w2_bytes, e_codes, e_bytes, first=False)
 
-        w3_bf = sb("w3_bf", [P, N * PACK], BF16)
+        w3_bf = sb("w3_bf", [P, N * PACK], BF16, tag="w3_then_fetched")
         nc.vector.tensor_tensor(
-            w3_bf[:].rearrange("p (c i j) -> p c j i", i=4, j=PACK),
-            w3_raw[:].rearrange("p j (c i) -> p c j i", i=4),
-            unit_sign[:].unsqueeze(1).unsqueeze(3).broadcast_to([P, N // 4, PACK, 4]),
+            woven(w3_bf),
+            by_pairs(w3_raw[:]),
+            unit_sign[:].unsqueeze(1).unsqueeze(3).broadcast_to([P, N // 2, PACK, 2]),
             ALU.mult,
         )
         w3_codes = sb("w3_codes", [P, N], U32)
@@ -141,34 +145,40 @@ def tile_picked_ysaecr_rec_p_kernel(
         nc.vector.quantize_mx(out=w3_codes[:].bitcast(FP8X4), scales=w3_bytes[:], in_=w3_bf[:])
 
         rival = sb("rival", [P, PACK * S], F32)
-
-        def rival_at(t):
-            return (PACK - 1 - t) * S
-
-        own = sb("own", [P, PACK, S], F32)
         fetched = sb("fetched", [P, PACK, S], F32, tag="w3_then_fetched")
         for bank, (t, lo, hi) in zip(banks, pieces):
-            nc.scalar.activation(rival[:, rival_at(t) + lo : rival_at(t) + hi], bank[:], ACT.Relu, bias=mate_bias[:, t : t + 1], scale=mate_scale[:, t : t + 1])
-        for bank, (t, lo, hi) in zip(banks, pieces):
-            nc.scalar.activation(own[:, t, lo:hi], bank[:], ACT.Relu, bias=own_bias[:, t : t + 1], scale=own_scale[:, t : t + 1])
-        for t, lo, hi in pieces:
-            window = rival[:, rival_at(t) : rival_at(t) + 2 * (hi - lo)]
-            nc.vector.tensor_copy(fetched[:, t, lo:hi], window.indirect(entries(fold_sb, lo, hi)))
+            nc.scalar.activation(
+                rival[:, t * S + lo : t * S + hi],
+                bank[:],
+                ACT.Relu,
+                bias=rival_bias[:, t : t + 1],
+                scale=rival_scale[:, t : t + 1],
+            )
+
+        rival_planes = rival[:].rearrange("p (t n) -> p t n", t=PACK)
+        own_upper = sb("own_upper", [P, PACK, HALF], F32)
+        nc.scalar.activation(own_upper[:], rival_planes[:, :, HALF:], ACT.Copy, scale=UNDO_PARTNER)
+        own_lower = sb("own_lower", [P, HALF * PACK], BF16, tag="own_lower_then_codes")
+        nc.scalar.activation(woven(own_lower), by_pairs(rival_planes[:, :, :HALF]), ACT.Copy, scale=UNDO_PARTNER)
+
+        for t in reversed(range(PACK)):
+            for lo, hi in (LOWER, UPPER) if t in (PACK - 1, 0) else (WHOLE,):
+                window = rival[:, t * S : t * S + 2 * (hi - lo)]
+                nc.vector.tensor_copy(fetched[:, t, lo:hi], window.indirect(entries(fold_sb, lo, hi)))
+        fetched_lower = sb("fetched_lower", [P, HALF * PACK], BF16)
+        nc.scalar.copy(woven(fetched_lower), by_pairs(fetched[:, :, :HALF]))
+
+        hid_upper = sb("hid_upper", [P, HALF * PACK], BF16)
+        hid_lower = sb("hid_lower", [P, HALF * PACK], BF16)
+        nc.vector.tensor_tensor(woven(hid_upper), by_pairs(fetched[:, :, HALF:]), by_pairs(own_upper[:]), ALU.max)
+        nc.vector.tensor_tensor(hid_lower[:], fetched_lower[:], own_lower[:], ALU.max)
 
         rebuilt = []
-        for c, (lo, hi) in enumerate(CHUNKS):
-            n = hi - lo
-            hid_bf = sb("hid_bf%d" % c, [P, n * PACK], BF16)
-            nc.vector.tensor_tensor(
-                hid_bf[:].rearrange("p (c i t) -> p c t i", i=4, t=PACK),
-                fetched[:, :, lo:hi].rearrange("p t (c i) -> p c t i", i=4),
-                own[:, :, lo:hi].rearrange("p t (c i) -> p c t i", i=4),
-                ALU.max,
-            )
-            hid_codes = sb("hid_codes%d" % c, [P, n], U32)
-            hid_bytes = sb("hid_bytes%d" % c, [P, n], U8)
+        for name, hid_bf, codes_tag in (("upper", hid_upper, "own_lower_then_codes"), ("lower", hid_lower, None)):
+            hid_codes = sb("hid_codes_" + name, [P, HALF], U32, tag=codes_tag)
+            hid_bytes = sb("hid_bytes_" + name, [P, HALF], U8)
             nc.vector.quantize_mx(out=hid_codes[:].bitcast(FP8X4), scales=hid_bytes[:], in_=hid_bf[:])
-            rr = psum.tile([P, n], F32, name="rr%d" % c)
+            rr = psum.tile([P, HALF], F32, name="rr_" + name)
             nc.tensor.matmul_mx(
                 out=rr[:],
                 lhsT=w3_codes[:].bitcast(FP8X4),
@@ -180,13 +190,11 @@ def tile_picked_ysaecr_rec_p_kernel(
             )
             rebuilt.append(rr)
 
-        for c, (lo, hi) in enumerate(CHUNKS):
-            n = hi - lo
-            rr = rebuilt[c]
-            err = sb("err%d" % c, [P, n], F32)
-            size = sb("size%d" % c, [P, n], F32)
-            result = sb("result%d" % c, [P, n], F32)
+        for name, rr, (lo, hi) in zip(("upper", "lower"), rebuilt, (UPPER, LOWER)):
+            err = sb("err_" + name, [P, HALF], F32)
+            abs_err = sb("abs_err_" + name, [P, HALF], F32)
+            result = sb("result_" + name, [P, HALF], F32)
             nc.vector.scalar_tensor_tensor(err[:], rr[:], -1.0, tgt_sb[:, lo:hi], ALU.mult, ALU.add)
-            nc.scalar.activation(size[:], err[:], ACT.Abs)
-            nc.vector.scalar_tensor_tensor(result[:], rr[:], -0.3, size[:], ALU.mult, ALU.add)
+            nc.scalar.activation(abs_err[:], err[:], ACT.Abs)
+            nc.vector.scalar_tensor_tensor(result[:], rr[:], -REBUILT, abs_err[:], ALU.mult, ALU.add)
             nc.sync.dma_start(out[:, lo:hi], result[:])

@@ -74,8 +74,8 @@ def tile_picked_ysaecr_rec_p_kernel(
         nc.sync.dma_start(fold_sb[:], fold)
         load_scale_rows(e_plane, e_scales)
         nc.sync.dma_start(w2_raw[:], w2.rearrange("(p j) c -> p j c", j=PACK))
-        nc.gpsimd.dma_start(unit_sb[:], unit.rearrange("(p t) o -> p (t o)", t=PACK))
-        nc.gpsimd.dma_start(thr_sb[:], thr.rearrange("(p t) o -> p (t o)", t=PACK))
+        nc.sync.dma_start(unit_sb[:], unit.rearrange("(p t) o -> p (t o)", t=PACK))
+        nc.sync.dma_start(thr_sb[:], thr.rearrange("(p t) o -> p (t o)", t=PACK))
 
         rival_scale = sb("rival_scale", [P, PACK], F32)
         unit_sign = sb("unit_sign", [P, PACK], F32)

from contextlib import ExitStack

import concourse.mybir as mybir

F32 = mybir.dt.float32
BF16 = mybir.dt.bfloat16
I32 = mybir.dt.int32
U32 = mybir.dt.uint32
U16 = mybir.dt.uint16
U8 = mybir.dt.uint8
FP8X4 = mybir.dt.float8_e4m3fn_x4
ALU = mybir.AluOpType
ACT = mybir.ActivationFunctionType

K, T, S, N, H, W = 512, 1024, 512, 128, 512, 2048
FLOPS = 2 * K * H * S * 2 + 2 * H * N * S

P = 128
PACK = 4
QUADRANTS = 4
LIST_ROWS = 16
HALF = S // 2
LOWER, UPPER, WHOLE = (0, HALF), (HALF, S), (0, S)
PARTNER = 0.8
UNDO_PARTNER = 1.25
REBUILT = 0.3


def tile_picked_ysaecr_rec_p_kernel(
    tc, x_words, x_scales, w1, e_words, e_scales, w2, thr, unit, w3, tgt, offs, mate, fold, out
):
    nc = tc.nc
    with ExitStack() as ctx:
        keep = ctx.enter_context(tc.tile_pool(name="keep", bufs=1))
        psum = ctx.enter_context(tc.psum_pool(name="psum", bufs=1))

        def sb(name, shape, dtype, tag=None):
            return keep.tile(shape, dtype, name=name, tag=tag or name, align_bytes=64)

        def entries(list_tile, lo, hi):
            return list_tile[:, lo // LIST_ROWS : hi // LIST_ROWS]

        def load_words(table, words):
            nc.sync.dma_start(table[:].bitcast(I32), words[0].rearrange("p n j -> p (n j)").bitcast(I32))

        def load_scale_rows(plane, rows):
            for q in range(QUADRANTS):
                nc.sync.dma_start(plane[32 * q : 32 * q + 4, :].bitcast(I32), rows[0, 4 * q : 4 * q + 4, :].bitcast(I32))

        def by_pairs(planes):
            return planes.rearrange("p t (c i) -> p c t i", i=2)

        def woven(tile):
            return tile[:].rearrange("p (c i t) -> p c t i", i=2, t=PACK)

        x_plane = sb("x_plane", [P, T], U8)
        e_plane = sb("e_plane", [P, W], U8)
        nc.gpsimd.memset(x_plane[:].bitcast(I32), 0)
        nc.vector.memset(e_plane[:].bitcast(I32), 0)

        offs_sb = keep.tile([P, S // LIST_ROWS], U16, name="offs_sb")
        mate_sb = keep.tile([P, S // LIST_ROWS], U16, name="mate_sb")
        fold_sb = keep.tile([P, S // LIST_ROWS], U16, name="fold_sb")
        unit_sb = sb("unit_sb", [P, PACK], F32)
        thr_sb = sb("thr_sb", [P, PACK], F32)
        w1_raw = sb("w1_raw", [P, PACK, H], F32, tag="w1_then_w3")
        w2_raw = sb("w2_raw", [P, PACK, H], F32, tag="w2_then_tgt")
        x_table = sb("x_table", [P, T], U32, tag="x_then_e")
        load_words(x_table, x_words)
        nc.sync.dma_start(offs_sb[:], offs)
        nc.sync.dma_start(mate_sb[:], mate)
        load_scale_rows(x_plane, x_scales)
        nc.sync.dma_start(w1_raw[:], w1.rearrange("(p j) c -> p j c", j=PACK))
        nc.sync.dma_start(fold_sb[:], fold)
        load_scale_rows(e_plane, e_scales)
        nc.sync.dma_start(w2_raw[:], w2.rearrange("(p j) c -> p j c", j=PACK))
        nc.sync.dma_start(unit_sb[:], unit.rearrange("(p t) o -> p (t o)", t=PACK))
        nc.sync.dma_start(thr_sb[:], thr.rearrange("(p t) o -> p (t o)", t=PACK))

        rival_scale = sb("rival_scale", [P, PACK], F32)
        unit_sign = sb("unit_sign", [P, PACK], F32)
        rival_bias = sb("rival_bias", [P, PACK], F32)
        nc.scalar.activation(rival_scale[:], unit_sb[:], ACT.Abs, scale=PARTNER)
        nc.scalar.activation(unit_sign[:], unit_sb[:], ACT.Sign)
        nc.gpsimd.tensor_tensor(rival_bias[:], rival_scale[:], thr_sb[:], ALU.mult)

        x_codes = sb("x_codes", [P, S], U32)
        x_bytes = sb("x_bytes", [P, S], U8)
        e_codes = sb("e_codes", [P, S], U32)
        e_bytes = sb("e_bytes", [P, S], U8)
        nc.vector.tensor_copy(x_codes[:], x_table[:].indirect(offs_sb[:]))
        e_table = sb("e_table", [P, W], U32, tag="x_then_e")
        load_words(e_table, e_words)
        nc.vector.tensor_copy(x_bytes[:], x_plane[:].indirect(offs_sb[:]))

        def quantize_encoder(name, raw):
            codes = sb(name + "_codes", [P, H], U32)
            scale_bytes = sb(name + "_bytes", [P, H], U8)
            dealt = raw[:].rearrange("p j (m t) -> p m j t", t=PACK)
            for pair, cast in ((1, nc.vector.tensor_copy), (0, nc.scalar.copy)):
                rounded = sb("%s_bf%d" % (name, pair), [P, 2 * H], BF16)
                cast(rounded[:].rearrange("p (t m j) -> p m j t", t=2, j=PACK), dealt[:, :, :, 2 * pair : 2 * pair + 2])
                cols = slice(pair * H // 2, (pair + 1) * H // 2)
                nc.vector.quantize_mx(out=codes[:, cols].bitcast(FP8X4), scales=scale_bytes[:, cols], in_=rounded[:])
            return codes, scale_bytes

        w1_codes, w1_bytes = quantize_encoder("w1", w1_raw)
        w3_raw = sb("w3_raw", [P, PACK, N], F32, tag="w1_then_w3")
        nc.sync.dma_start(w3_raw[:], w3.rearrange("(p j) n -> p j n", j=PACK))
        w2_codes, w2_bytes = quantize_encoder("w2", w2_raw)
        tgt_sb = sb("tgt_sb", [P, S], F32, tag="w2_then_tgt")
        nc.sync.dma_start(tgt_sb[:], tgt)
        nc.vector.tensor_copy(e_bytes[:], e_plane[:].indirect(mate_sb[:]))

        pieces = [(PACK - 1, *LOWER), (PACK - 1, *UPPER)] + [(t, *WHOLE) for t in reversed(range(PACK - 1))]
        banks = [psum.tile([P, hi - lo], F32, name="z%d" % i) for i, (t, lo, hi) in enumerate(pieces)]

        def encode(w_codes, w_bytes, codes, scale_bytes, first):
            for bank, (t, lo, hi) in zip(banks, pieces):
                latents = slice(t * P, (t + 1) * P)
                nc.tensor.matmul_mx(
                    out=bank[:],
                    lhsT=w_codes[:, latents].bitcast(FP8X4),
                    lhsT_scale=w_bytes[:, latents],
                    rhs=codes[:, lo:hi].bitcast(FP8X4),
                    rhs_scale=scale_bytes[:, lo:hi],
                    start=first,
                    stop=not first,
                )

        encode(w1_codes, w1_bytes, x_codes, x_bytes, first=True)
        for lo, hi in (LOWER, UPPER):
            nc.vector.tensor_copy(e_codes[:, lo:hi], e_table[:].indirect(entries(mate_sb, lo, hi)))
        encode(w2_codes, w2_bytes, e_codes, e_bytes, first=False)

        w3_bf = sb("w3_bf", [P, N * PACK], BF16, tag="w3_then_fetched")
        nc.vector.tensor_tensor(
            woven(w3_bf),
            by_pairs(w3_raw[:]),
            unit_sign[:].unsqueeze(1).unsqueeze(3).broadcast_to([P, N // 2, PACK, 2]),
            ALU.mult,
        )
        w3_codes = sb("w3_codes", [P, N], U32)
        w3_bytes = sb("w3_bytes", [P, N], U8)
        nc.vector.quantize_mx(out=w3_codes[:].bitcast(FP8X4), scales=w3_bytes[:], in_=w3_bf[:])

        rival = sb("rival", [P, PACK * S], F32)
        fetched = sb("fetched", [P, PACK, S], F32, tag="w3_then_fetched")
        for bank, (t, lo, hi) in zip(banks, pieces):
            nc.scalar.activation(
                rival[:, t * S + lo : t * S + hi],
                bank[:],
                ACT.Relu,
                bias=rival_bias[:, t : t + 1],
                scale=rival_scale[:, t : t + 1],
            )

        rival_planes = rival[:].rearrange("p (t n) -> p t n", t=PACK)
        own_upper = sb("own_upper", [P, PACK, HALF], F32)
        nc.scalar.activation(own_upper[:], rival_planes[:, :, HALF:], ACT.Copy, scale=UNDO_PARTNER)
        own_lower = sb("own_lower", [P, HALF * PACK], BF16, tag="own_lower_then_codes")
        nc.scalar.activation(woven(own_lower), by_pairs(rival_planes[:, :, :HALF]), ACT.Copy, scale=UNDO_PARTNER)

        for t in reversed(range(PACK)):
            for lo, hi in (LOWER, UPPER) if t in (PACK - 1, 0) else (WHOLE,):
                window = rival[:, t * S : t * S + 2 * (hi - lo)]
                nc.vector.tensor_copy(fetched[:, t, lo:hi], window.indirect(entries(fold_sb, lo, hi)))
        fetched_lower = sb("fetched_lower", [P, HALF * PACK], BF16)
        nc.scalar.copy(woven(fetched_lower), by_pairs(fetched[:, :, :HALF]))

        hid_upper = sb("hid_upper", [P, HALF * PACK], BF16)
        hid_lower = sb("hid_lower", [P, HALF * PACK], BF16)
        nc.vector.tensor_tensor(woven(hid_upper), by_pairs(fetched[:, :, HALF:]), by_pairs(own_upper[:]), ALU.max)
        nc.vector.tensor_tensor(hid_lower[:], fetched_lower[:], own_lower[:], ALU.max)

        rebuilt = []
        for name, hid_bf, codes_tag in (("upper", hid_upper, "own_lower_then_codes"), ("lower", hid_lower, None)):
            hid_codes = sb("hid_codes_" + name, [P, HALF], U32, tag=codes_tag)
            hid_bytes = sb("hid_bytes_" + name, [P, HALF], U8)
            nc.vector.quantize_mx(out=hid_codes[:].bitcast(FP8X4), scales=hid_bytes[:], in_=hid_bf[:])
            rr = psum.tile([P, HALF], F32, name="rr_" + name)
            nc.tensor.matmul_mx(
                out=rr[:],
                lhsT=w3_codes[:].bitcast(FP8X4),
                lhsT_scale=w3_bytes[:],
                rhs=hid_codes[:].bitcast(FP8X4),
                rhs_scale=hid_bytes[:],
                start=True,
                stop=True,
            )
            rebuilt.append(rr)

        for name, rr, (lo, hi) in zip(("upper", "lower"), rebuilt, (UPPER, LOWER)):
            err = sb("err_" + name, [P, HALF], F32)
            abs_err = sb("abs_err_" + name, [P, HALF], F32)
            result = sb("result_" + name, [P, HALF], F32)
            nc.vector.scalar_tensor_tensor(err[:], rr[:], -1.0, tgt_sb[:, lo:hi], ALU.mult, ALU.add)
            nc.scalar.activation(abs_err[:], err[:], ACT.Abs)
            nc.vector.scalar_tensor_tensor(result[:], rr[:], -REBUILT, abs_err[:], ALU.mult, ALU.add)
            nc.sync.dma_start(out[:, lo:hi], result[:])
